import numpy as np
import ml_dtypes


def mxq(x, axis, fmt="e4m3"):
    dtype, down = {"e4m3": (ml_dtypes.float8_e4m3fn, 7), "e5m2": (ml_dtypes.float8_e5m2, 14)}[fmt]
    v = np.moveaxis(np.asarray(x, np.float32).astype(ml_dtypes.bfloat16).astype(np.float64), axis, -1)
    blocks = v.reshape(v.shape[:-1] + (-1, 32))
    amax = np.abs(blocks).max(-1, keepdims=True)
    byte = np.maximum(np.where(amax > 0, np.frexp(amax)[1] - 1 + 127, 0) - down, 1)
    scale = np.exp2(byte - 127.0)
    codes = (blocks / scale).astype(np.float32).astype(dtype).astype(np.float64)
    return np.moveaxis((codes * scale).reshape(v.shape), -1, axis)


WIDE = False


def mx_kscale(k):
    if not WIDE:
        return np.ones(k)
    levels = np.array([30, -30])
    if k % 512:
        return np.exp2(np.random.permutation(np.resize(levels, k // 32))).repeat(32)
    a = np.empty((k // 512, 16))
    for p in range(k // 512):
        a[p, :8] = np.random.permutation(np.resize(levels, 8))
        for g in range(8):
            far = levels[np.abs(levels - a[p, g]) >= 10]
            a[p, g + 8] = far[np.random.randint(len(far))]
    return np.exp2(a.ravel()).repeat(32)


def f64(x):
    return np.asarray(x).astype(np.float64)


def striped(idx):
    return np.tile(np.asarray(idx).reshape(-1, 16).T, (8, 1)).astype(np.uint16)


def unstriped(offs):
    return offs[:16].T.reshape(-1).astype(np.int64)


K, J, N, T, V, C, Q = 256, 1024, 256, 2048, 2048, 128, 1024


def setup_inputs():
    n = np.random.standard_normal
    idx = np.random.permutation(T)[:J]
    idx2 = np.random.permutation(V)[:J]
    idx3 = np.random.permutation(Q)[:N]
    fj = mx_kscale(J)
    return {
        "xf": (n((K, T))).astype(np.float32),
        "ra": (np.random.uniform(0.5, 1.5, (1, J)) * fj).astype(np.float32),
        "ow": (n((K, J)) * 0.7).astype(np.float32),
        "gt": (n((N, V)) * np.exp(0.5 * n((1, V)))).astype(np.float32),
        "rb": (np.random.uniform(0.5, 1.5, (1, J)) / fj).astype(np.float32),
        "old": (0.5 * n((K, Q))).astype(np.float32),
        "offs": striped(idx),
        "offs2": striped(idx2),
        "offs3": striped(idx3),
    }


def reference(xf, ra, ow, gt, rb, old, offs, offs2, offs3):
    idx = unstriped(offs)
    idx2 = unstriped(offs2)
    idx3 = unstriped(offs3)
    us = (f64(xf)[:, idx] - f64(ow)) * f64(ra)
    uj = us.T
    gg = f64(gt)[:, idx2]
    c1 = gg.reshape(N, C, J // C).mean(axis=2)
    c2 = np.repeat(c1, J // C, axis=1)
    gs = (gg - c2) * f64(rb)
    gj = gs.T
    ujq = mxq(uj, 0, "e4m3")
    gjq = mxq(gj, 0, "e5m2")
    w = ujq.T @ gjq
    wp = np.zeros((K, Q))
    wp[:, idx3] = w
    y = 0.04 * wp + f64(old)
    return y

@@ -1,0 +1,183 @@
+from contextlib import ExitStack
+
+import concourse.mybir as mybir
+from concourse.masks import make_identity
+
+K, J, N, T, V, Q = 256, 1024, 256, 2048, 2048, 1024
+FLOPS = 2 * K * J * N
+
+F32 = mybir.dt.float32
+BF16 = mybir.dt.bfloat16
+U32 = mybir.dt.uint32
+U16 = mybir.dt.uint16
+U8 = mybir.dt.uint8
+E4M3X4 = mybir.dt.float8_e4m3fn_x4
+E5M2X4 = mybir.dt.float8_e5m2_x4
+ALU = mybir.AluOpType
+COPY = mybir.ActivationFunctionType.Copy
+
+P = 128
+PACK = 4
+J_PASS = P * PACK
+PASSES = J // J_PASS
+SET = 8
+BLOCKS = J_PASS // 32
+LIST_COLS = J_PASS // 16
+ALPHA = 0.04
+BANKS = 5
+
+
+def tile_list_moment_offset_centred_placed_kernel(tc, xf, ra, ow, gt, rb, old, offs, offs2, offs3, out):
+    nc = tc.nc
+    with ExitStack() as ctx:
+        keep = ctx.enter_context(tc.tile_pool(name="keep", bufs=1))
+        psum = ctx.enter_context(tc.psum_pool(name="psum", bufs=1))
+
+        def load(name, src, dtype=F32):
+            t = keep.tile(list(src.shape), dtype, name=name)
+            nc.sync.dma_start(t[:], src)
+            return t
+
+        def rows(i):
+            return slice(P * i, P * (i + 1))
+
+        g_list = load("g_list", offs2, U16)
+        g_table = [load("g_table%d" % i, gt[rows(i), :]) for i in range(2)]
+        x_list = load("x_list", offs, U16)
+        x_table = []
+        own = []
+        for i in range(2):
+            x_table.append(load("x_table%d" % i, xf[rows(i), :]))
+            own.append([load("own%d_%d" % (i, g), ow[rows(i), J_PASS * g : J_PASS * (g + 1)]) for g in range(PASSES)])
+        place_list = load("place_list", offs3, U16)
+        store_old = [load("store_old%d" % i, old[rows(i), :]) for i in range(2)]
+
+        ident = keep.tile([P, P], F32, name="ident")
+        make_identity(nc, ident[:])
+
+        w_rows = keep.tile([P, PASSES * P], F32, name="w_rows")
+        nc.gpsimd.memset(w_rows[:], 0.0)
+        for s, vec in enumerate((ra, rb)):
+            nc.gpsimd.dma_start(
+                w_rows[PACK * s : PACK * (s + 1), :].rearrange("t (b r) -> t b r", r=SET),
+                vec.rearrange("o (b t r) -> t (o b) r", t=PACK, r=SET),
+            )
+        w_bank = psum.tile([P, PASSES, P], F32, name="w_bank")
+        for g in range(PASSES):
+            nc.tensor.transpose(w_bank[:, g, :], w_rows[:, P * g : P * (g + 1)], ident[:])
+        slot_w = keep.tile([P, PASSES, 2 * PACK], F32, name="slot_w")
+        nc.vector.tensor_copy(slot_w[:], w_bank[:, :, 0 : 2 * PACK])
+
+        pages = []
+        for i in range(2):
+            page = keep.tile([P, Q], F32, name="page%d" % i)
+            nc.vector.memset(page[:], 0.0)
+            pages.append(page)
+
+        g_codes = [keep.tile([P, N], U32, name="g_codes%d" % g, align_bytes=64) for g in range(PASSES)]
+        g_scales = [keep.tile([P, N], U8, name="g_scales%d" % g, align_bytes=64) for g in range(PASSES)]
+        u_codes = {}
+        u_scales = {}
+
+        def gather(name, table, lst, g):
+            picked = keep.tile([P, J_PASS], F32, name=name)
+            nc.scalar.activation(picked[:], table[:].indirect(lst[:, LIST_COLS * g : LIST_COLS * (g + 1)]), COPY)
+            return picked
+
+        def by_slot(ap):
+            return ap.rearrange("p (b t r) -> p t b r", t=PACK, r=SET)
+
+        def slots(tile):
+            return tile[:].rearrange("p (t b r) -> p t b r", t=PACK, r=SET)
+
+        def centre(name, picked):
+            sums = keep.tile([P, J_PASS // SET], F32, name=name + "_sums")
+            nc.vector.tensor_reduce(sums[:], picked[:].rearrange("p (c r) -> p c r", r=SET), mybir.AxisListType.X, ALU.add)
+            means = keep.tile([P, J_PASS // SET], F32, name=name + "_means")
+            nc.vector.tensor_scalar(means[:], sums[:], 1.0 / SET, None, ALU.mult)
+            diff = keep.tile([P, J_PASS], F32, name=name)
+            spread = means[:].rearrange("p (b t o) -> p t b o", t=PACK, o=1).to_broadcast([P, PACK, BLOCKS, SET])
+            nc.vector.tensor_tensor(slots(diff), by_slot(picked[:]), spread, ALU.subtract)
+            return diff
+
+        def offset(name, picked, mine):
+            diff = keep.tile([P, J_PASS], F32, name=name)
+            nc.vector.tensor_tensor(slots(diff), by_slot(picked[:]), by_slot(mine[:]), ALU.subtract)
+            return diff
+
+        def turn(diff):
+            bank = psum.tile([P, PACK, P], F32, name="bank", tag="bank", bufs=BANKS)
+            for t in range(PACK):
+                nc.tensor.transpose(bank[:, t, :], diff[:, P * t : P * (t + 1)], ident[:])
+            return bank
+
+        def weigh(name, bank, g, side):
+            grouped = keep.tile([P, P, PACK], BF16, name=name, align_bytes=64)
+            wts = slot_w[:, g : g + 1, PACK * side : PACK * (side + 1)].to_broadcast([P, P, PACK])
+            nc.vector.tensor_tensor(grouped[:], bank[:].rearrange("p t n -> p n t"), wts, ALU.mult)
+            return grouped
+
+        def quantise(grouped, codes, scales):
+            nc.vector.quantize_mx(out=codes, scales=scales, in_=grouped[:].rearrange("p n t -> p (n t)"))
+
+        def moment(i):
+            acc = psum.tile([P, N], F32, name="acc%d" % i)
+            for g in range(PASSES):
+                nc.tensor.matmul_mx(
+                    out=acc[:],
+                    lhsT=u_codes[i, g][:].bitcast(E4M3X4),
+                    lhsT_scale=u_scales[i, g][:],
+                    rhs=g_codes[g][:].bitcast(E5M2X4),
+                    rhs_scale=g_scales[g][:],
+                    start=(g == 0),
+                    stop=(g == PASSES - 1),
+                )
+            w = keep.tile([P, N], F32, name="w%d" % i)
+            nc.scalar.activation(w[:], acc[:], COPY)
+            nc.scalar.activation(pages[i][:].indirect(place_list[:]), w[:], COPY)
+
+        def finish(i, pieces):
+            width = Q // pieces
+            for h in range(pieces):
+                cols = slice(width * h, width * (h + 1))
+                res = keep.tile([P, width], F32, name="res%d_%d" % (i, h))
+                nc.vector.scalar_tensor_tensor(res[:], pages[i][:, cols], ALPHA, store_old[i][:, cols], ALU.mult, ALU.add)
+                nc.sync.dma_start(out[rows(i), cols], res[:])
+
+        units = [("g", i, g) for i in range(2) for g in range(PASSES)] + [("x", i, g) for i in range(2) for g in range(PASSES)]
+        banks = {}
+        grouped = {}
+
+        def front(unit):
+            side, i, g = unit
+            name = "%s%d_%d" % unit
+            if side == "g":
+                diff = centre("centred_" + name, gather("picked_" + name, g_table[i], g_list, g))
+            else:
+                diff = offset("offset_" + name, gather("picked_" + name, x_table[i], x_list, g), own[i][g])
+            banks[unit] = turn(diff)
+
+        def middle(unit):
+            side, i, g = unit
+            grouped[unit] = weigh("grouped_%s%d_%d" % unit, banks[unit], g, 1 if side == "g" else 0)
+
+        def back(unit):
+            side, i, g = unit
+            if side == "g":
+                quantise(grouped[unit], g_codes[g][:, rows(i)].bitcast(E5M2X4), g_scales[g][:, rows(i)])
+            else:
+                u_codes[i, g] = keep.tile([P, P], U32, name="u_codes%d_%d" % (i, g), align_bytes=64)
+                u_scales[i, g] = keep.tile([P, P], U8, name="u_scales%d_%d" % (i, g), align_bytes=64)
+                quantise(grouped[unit], u_codes[i, g][:].bitcast(E4M3X4), u_scales[i, g][:])
+                if g == PASSES - 1:
+                    moment(i)
+
+        for step in range(len(units) + 2):
+            if step < len(units):
+                front(units[step])
+            if 2 <= step:
+                back(units[step - 2])
+            if 1 <= step <= len(units):
+                middle(units[step - 1])
+        finish(0, 1)
+        finish(1, 2)

@@ -25,6 +25,10 @@ BLOCKS = J_PASS // 32
 LIST_COLS = J_PASS // 16
 ALPHA = 0.04
 BANKS = 5
+V_GATHERS = [("g", 0, 0)]
+V_SUBS = [("g", 0, 0), ("x", 0, 1), ("x", 1, 0), ("x", 1, 1)]
+LAST = 1
+TAGS = {}
 
 
 def tile_list_moment_offset_centred_placed_kernel(tc, xf, ra, ow, gt, rb, old, offs, offs2, offs3, out):
@@ -32,6 +36,9 @@ def tile_list_moment_offset_centred_placed_kernel(tc, xf, ra, ow, gt, rb, old, o
     with ExitStack() as ctx:
         keep = ctx.enter_context(tc.tile_pool(name="keep", bufs=1))
         psum = ctx.enter_context(tc.psum_pool(name="psum", bufs=1))
+
+        def new(name, shape, dtype):
+            return keep.tile(shape, dtype, name=name, tag=TAGS.get(name, name), align_bytes=64)
 
         def load(name, src, dtype=F32):
             t = keep.tile(list(src.shape), dtype, name=name)
@@ -42,7 +49,15 @@ def tile_list_moment_offset_centred_placed_kernel(tc, xf, ra, ow, gt, rb, old, o
             return slice(P * i, P * (i + 1))
 
         g_list = load("g_list", offs2, U16)
-        g_table = [load("g_table%d" % i, gt[rows(i), :]) for i in range(2)]
+        g_table = [load("g_table0", gt[rows(0), :])]
+        w_rows = keep.tile([P, PASSES * P], F32, name="w_rows")
+        nc.vector.memset(w_rows[:], 0.0)
+        for s, vec in enumerate((ra, rb)):
+            nc.sync.dma_start(
+                w_rows[PACK * s : PACK * (s + 1), :].rearrange("t (b r) -> t b r", r=SET),
+                vec.rearrange("o (b t r) -> t (o b) r", t=PACK, r=SET),
+            )
+        g_table.append(load("g_table1", gt[rows(1), :]))
         x_list = load("x_list", offs, U16)
         x_table = []
         own = []
@@ -52,16 +67,14 @@ def tile_list_moment_offset_centred_placed_kernel(tc, xf, ra, ow, gt, rb, old, o
         place_list = load("place_list", offs3, U16)
         store_old = [load("store_old%d" % i, old[rows(i), :]) for i in range(2)]
 
+        warm_in = keep.tile([P, 1], F32, name="warm_in")
+        warm_out = keep.tile([P, 1], F32, name="warm_out")
+        nc.vector.memset(warm_in[:], 0.0)
+        nc.scalar.activation(warm_out[:], warm_in[:], COPY)
+
         ident = keep.tile([P, P], F32, name="ident")
         make_identity(nc, ident[:])
 
-        w_rows = keep.tile([P, PASSES * P], F32, name="w_rows")
-        nc.gpsimd.memset(w_rows[:], 0.0)
-        for s, vec in enumerate((ra, rb)):
-            nc.gpsimd.dma_start(
-                w_rows[PACK * s : PACK * (s + 1), :].rearrange("t (b r) -> t b r", r=SET),
-                vec.rearrange("o (b t r) -> t (o b) r", t=PACK, r=SET),
-            )
         w_bank = psum.tile([P, PASSES, P], F32, name="w_bank")
         for g in range(PASSES):
             nc.tensor.transpose(w_bank[:, g, :], w_rows[:, P * g : P * (g + 1)], ident[:])
@@ -74,14 +87,23 @@ def tile_list_moment_offset_centred_placed_kernel(tc, xf, ra, ow, gt, rb, old, o
             nc.vector.memset(page[:], 0.0)
             pages.append(page)
 
-        g_codes = [keep.tile([P, N], U32, name="g_codes%d" % g, align_bytes=64) for g in range(PASSES)]
-        g_scales = [keep.tile([P, N], U8, name="g_scales%d" % g, align_bytes=64) for g in range(PASSES)]
+        g_grouped = [new("g_grouped%d" % g, [P, N, PACK], BF16) for g in range(PASSES)]
+        g_codes = [new("g_codes%d" % g, [P, N], U32) for g in range(PASSES)]
+        g_scales = [new("g_scales%d" % g, [P, N], U8) for g in range(PASSES)]
+        res0 = new("res0", [P, Q], F32)
+        late_diff = [new("late_diff%d" % g, [P, J_PASS], F32) for g in range(PASSES)]
+        bank_ring = [psum.tile([P, PACK, P], F32, name="bank%d" % b) for b in range(4)]
+        turned = []
         u_codes = {}
         u_scales = {}
 
-        def gather(name, table, lst, g):
-            picked = keep.tile([P, J_PASS], F32, name=name)
-            nc.scalar.activation(picked[:], table[:].indirect(lst[:, LIST_COLS * g : LIST_COLS * (g + 1)]), COPY)
+        def gather(name, table, lst, g, on_vector):
+            picked = new(name, [P, J_PASS], F32)
+            listed = table[:].indirect(lst[:, LIST_COLS * g : LIST_COLS * (g + 1)])
+            if on_vector:
+                nc.vector.tensor_copy(picked[:], listed)
+            else:
+                nc.scalar.activation(picked[:], listed, COPY)
             return picked
 
         def by_slot(ap):
@@ -90,35 +112,33 @@ def tile_list_moment_offset_centred_placed_kernel(tc, xf, ra, ow, gt, rb, old, o
         def slots(tile):
             return tile[:].rearrange("p (t b r) -> p t b r", t=PACK, r=SET)
 
-        def centre(name, picked):
-            sums = keep.tile([P, J_PASS // SET], F32, name=name + "_sums")
+        def centre(name, picked, eng):
+            sums = new(name + "_sums", [P, J_PASS // SET], F32)
             nc.vector.tensor_reduce(sums[:], picked[:].rearrange("p (c r) -> p c r", r=SET), mybir.AxisListType.X, ALU.add)
-            means = keep.tile([P, J_PASS // SET], F32, name=name + "_means")
-            nc.vector.tensor_scalar(means[:], sums[:], 1.0 / SET, None, ALU.mult)
-            diff = keep.tile([P, J_PASS], F32, name=name)
+            means = new(name + "_means", [P, J_PASS // SET], F32)
+            eng.tensor_scalar(means[:], sums[:], 1.0 / SET, 0.0, ALU.mult, ALU.add)
+            diff = new(name, [P, J_PASS], F32)
             spread = means[:].rearrange("p (b t o) -> p t b o", t=PACK, o=1).to_broadcast([P, PACK, BLOCKS, SET])
-            nc.vector.tensor_tensor(slots(diff), by_slot(picked[:]), spread, ALU.subtract)
+            eng.tensor_tensor(slots(diff), by_slot(picked[:]), spread, ALU.subtract)
             return diff
 
-        def offset(name, picked, mine):
-            diff = keep.tile([P, J_PASS], F32, name=name)
-            nc.vector.tensor_tensor(slots(diff), by_slot(picked[:]), by_slot(mine[:]), ALU.subtract)
+        def offset(diff, picked, mine, eng):
+            eng.tensor_tensor(slots(diff), by_slot(picked[:]), by_slot(mine[:]), ALU.subtract)
             return diff
 
         def turn(diff):
-            bank = psum.tile([P, PACK, P], F32, name="bank", tag="bank", bufs=BANKS)
+            bank = bank_ring[len(turned) % len(bank_ring)]
+            turned.append(diff)
             for t in range(PACK):
                 nc.tensor.transpose(bank[:, t, :], diff[:, P * t : P * (t + 1)], ident[:])
             return bank
 
-        def weigh(name, bank, g, side):
-            grouped = keep.tile([P, P, PACK], BF16, name=name, align_bytes=64)
+        def weigh(grouped, bank, g, side):
             wts = slot_w[:, g : g + 1, PACK * side : PACK * (side + 1)].to_broadcast([P, P, PACK])
-            nc.vector.tensor_tensor(grouped[:], bank[:].rearrange("p t n -> p n t"), wts, ALU.mult)
-            return grouped
+            nc.vector.tensor_tensor(grouped, bank[:].rearrange("p t n -> p n t"), wts, ALU.mult)
 
         def quantise(grouped, codes, scales):
-            nc.vector.quantize_mx(out=codes, scales=scales, in_=grouped[:].rearrange("p n t -> p (n t)"))
+            nc.vector.quantize_mx(out=codes, scales=scales, in_=grouped.rearrange("p n t -> p (n t)"))
 
         def moment(i):
             acc = psum.tile([P, N], F32, name="acc%d" % i)
@@ -136,48 +156,67 @@ def tile_list_moment_offset_centred_placed_kernel(tc, xf, ra, ow, gt, rb, old, o
             nc.scalar.activation(w[:], acc[:], COPY)
             nc.scalar.activation(pages[i][:].indirect(place_list[:]), w[:], COPY)
 
-        def finish(i, pieces):
-            width = Q // pieces
-            for h in range(pieces):
-                cols = slice(width * h, width * (h + 1))
-                res = keep.tile([P, width], F32, name="res%d_%d" % (i, h))
+        def finish(i, widths):
+            c0 = 0
+            for h, width in enumerate(widths):
+                cols = slice(c0, c0 + width)
+                c0 = c0 + width
+                res = res0 if i == 0 else new("res%d_%d" % (i, h), [P, width], F32)
                 nc.vector.scalar_tensor_tensor(res[:], pages[i][:, cols], ALPHA, store_old[i][:, cols], ALU.mult, ALU.add)
                 nc.sync.dma_start(out[rows(i), cols], res[:])
 
-        units = [("g", i, g) for i in range(2) for g in range(PASSES)] + [("x", i, g) for i in range(2) for g in range(PASSES)]
         banks = {}
         grouped = {}
 
-        def front(unit):
-            side, i, g = unit
-            name = "%s%d_%d" % unit
+        def front(side, i, g):
+            unit = (side, i, g)
+            name = "%s%d%d" % unit
+            eng = nc.vector if unit in V_SUBS else nc.gpsimd
             if side == "g":
-                diff = centre("centred_" + name, gather("picked_" + name, g_table[i], g_list, g))
+                diff = centre("diff_" + name, gather("picked_" + name, g_table[i], g_list, g, unit in V_GATHERS), eng)
             else:
-                diff = offset("offset_" + name, gather("picked_" + name, x_table[i], x_list, g), own[i][g])
+                diff = offset(late_diff[g] if i == 1 else new("diff_" + name, [P, J_PASS], F32), gather("picked_" + name, x_table[i], x_list, g, unit in V_GATHERS), own[i][g], eng)
             banks[unit] = turn(diff)
 
-        def middle(unit):
-            side, i, g = unit
-            grouped[unit] = weigh("grouped_%s%d_%d" % unit, banks[unit], g, 1 if side == "g" else 0)
-
-        def back(unit):
-            side, i, g = unit
+        def middle(side, i, g):
             if side == "g":
-                quantise(grouped[unit], g_codes[g][:, rows(i)].bitcast(E5M2X4), g_scales[g][:, rows(i)])
+                weigh(g_grouped[g][:, rows(i), :], banks[side, i, g], g, 1)
             else:
-                u_codes[i, g] = keep.tile([P, P], U32, name="u_codes%d_%d" % (i, g), align_bytes=64)
-                u_scales[i, g] = keep.tile([P, P], U8, name="u_scales%d_%d" % (i, g), align_bytes=64)
-                quantise(grouped[unit], u_codes[i, g][:].bitcast(E4M3X4), u_scales[i, g][:])
-                if g == PASSES - 1:
-                    moment(i)
+                host = late_diff[1 - g] if i == 0 else (res0 if g == LAST else new("grouped_x1", [P, J_PASS // 2], F32))
+                grouped[i, g] = host[:, 0 : J_PASS // 2].bitcast(BF16).rearrange("p (n t) -> p n t", t=PACK)
+                weigh(grouped[i, g], banks[side, i, g], g, 0)
 
-        for step in range(len(units) + 2):
-            if step < len(units):
-                front(units[step])
-            if 2 <= step:
-                back(units[step - 2])
-            if 1 <= step <= len(units):
-                middle(units[step - 1])
-        finish(0, 1)
-        finish(1, 2)
+        def back_g(g):
+            quantise(g_grouped[g][:], g_codes[g][:].bitcast(E5M2X4), g_scales[g][:])
+
+        def back_x(i, g):
+            u_codes[i, g] = new("u_codes%d_%d" % (i, g), [P, P], U32)
+            u_scales[i, g] = new("u_scales%d_%d" % (i, g), [P, P], U8)
+            quantise(grouped[i, g], u_codes[i, g][:].bitcast(E4M3X4), u_scales[i, g][:])
+
+        front("g", 0, 0)
+        front("g", 0, 1)
+        front("g", 1, 0)
+        middle("g", 0, 0)
+        front("g", 1, 1)
+        middle("g", 0, 1)
+        front("x", 0, 0)
+        middle("g", 1, 0)
+        front("x", 0, 1)
+        back_g(0)
+        middle("g", 1, 1)
+        middle("x", 0, 1)
+        back_g(1)
+        middle("x", 0, 0)
+        back_x(0, 1)
+        front("x", 1, 0)
+        back_x(0, 0)
+        moment(0)
+        front("x", 1, 1)
+        middle("x", 1, 0)
+        middle("x", 1, 1)
+        back_x(1, 0)
+        back_x(1, 1)
+        moment(1)
+        finish(0, [1024])
+        finish(1, [512, 256, 256])

@@ -26,8 +26,7 @@ LIST_COLS = J_PASS // 16
 ALPHA = 0.04
 BANKS = 5
 V_GATHERS = [("g", 0, 0)]
-V_SUBS = [("g", 0, 0), ("x", 0, 1), ("x", 1, 0), ("x", 1, 1)]
-LAST = 1
+V_SUBS = [("g", 0, 1), ("g", 1, 1)]
 TAGS = {}
 
 
@@ -41,7 +40,7 @@ def tile_list_moment_offset_centred_placed_kernel(tc, xf, ra, ow, gt, rb, old, o
             return keep.tile(shape, dtype, name=name, tag=TAGS.get(name, name), align_bytes=64)
 
         def load(name, src, dtype=F32):
-            t = keep.tile(list(src.shape), dtype, name=name)
+            t = keep.tile(list(src.shape), dtype, name=name, align_bytes=64)
             nc.sync.dma_start(t[:], src)
             return t
 
@@ -59,11 +58,14 @@ def tile_list_moment_offset_centred_placed_kernel(tc, xf, ra, ow, gt, rb, old, o
             )
         g_table.append(load("g_table1", gt[rows(1), :]))
         x_list = load("x_list", offs, U16)
-        x_table = []
-        own = []
-        for i in range(2):
-            x_table.append(load("x_table%d" % i, xf[rows(i), :]))
-            own.append([load("own%d_%d" % (i, g), ow[rows(i), J_PASS * g : J_PASS * (g + 1)]) for g in range(PASSES)])
+        def load_own(i, g):
+            return load("own%d_%d" % (i, g), ow[rows(i), J_PASS * g : J_PASS * (g + 1)])
+
+        x_table = [load("x_table0", xf[rows(0), :])]
+        own = [[load_own(0, 0)]]
+        x_table.append(load("x_table1", xf[rows(1), :]))
+        own[0].append(load_own(0, 1))
+        own.append([load_own(1, g) for g in range(PASSES)])
         place_list = load("place_list", offs3, U16)
         store_old = [load("store_old%d" % i, old[rows(i), :]) for i in range(2)]
 
@@ -91,7 +93,6 @@ def tile_list_moment_offset_centred_placed_kernel(tc, xf, ra, ow, gt, rb, old, o
         g_codes = [new("g_codes%d" % g, [P, N], U32) for g in range(PASSES)]
         g_scales = [new("g_scales%d" % g, [P, N], U8) for g in range(PASSES)]
         res0 = new("res0", [P, Q], F32)
-        late_diff = [new("late_diff%d" % g, [P, J_PASS], F32) for g in range(PASSES)]
         bank_ring = [psum.tile([P, PACK, P], F32, name="bank%d" % b) for b in range(4)]
         turned = []
         u_codes = {}
@@ -175,14 +176,14 @@ def tile_list_moment_offset_centred_placed_kernel(tc, xf, ra, ow, gt, rb, old, o
             if side == "g":
                 diff = centre("diff_" + name, gather("picked_" + name, g_table[i], g_list, g, unit in V_GATHERS), eng)
             else:
-                diff = offset(late_diff[g] if i == 1 else new("diff_" + name, [P, J_PASS], F32), gather("picked_" + name, x_table[i], x_list, g, unit in V_GATHERS), own[i][g], eng)
+                diff = offset(new("diff_" + name, [P, J_PASS], F32), gather("picked_" + name, x_table[i], x_list, g, unit in V_GATHERS), own[i][g], eng)
             banks[unit] = turn(diff)
 
         def middle(side, i, g):
             if side == "g":
                 weigh(g_grouped[g][:, rows(i), :], banks[side, i, g], g, 1)
             else:
-                host = late_diff[1 - g] if i == 0 else (res0 if g == LAST else new("grouped_x1", [P, J_PASS // 2], F32))
+                host = new("grouped_x%d%d" % (i, g), [P, J_PASS // 2], F32) if (i, g) != (1, 1) else res0
                 grouped[i, g] = host[:, 0 : J_PASS // 2].bitcast(BF16).rearrange("p (n t) -> p n t", t=PACK)
                 weigh(grouped[i, g], banks[side, i, g], g, 0)
 
@@ -197,25 +198,25 @@ def tile_list_moment_offset_centred_placed_kernel(tc, xf, ra, ow, gt, rb, old, o
         front("g", 0, 0)
         front("g", 0, 1)
         front("g", 1, 0)
+        middle("g", 0, 1)
         middle("g", 0, 0)
         front("g", 1, 1)
-        middle("g", 0, 1)
         front("x", 0, 0)
         middle("g", 1, 0)
-        front("x", 0, 1)
         back_g(0)
+        front("x", 0, 1)
         middle("g", 1, 1)
-        middle("x", 0, 1)
-        back_g(1)
         middle("x", 0, 0)
-        back_x(0, 1)
-        front("x", 1, 0)
+        back_g(1)
         back_x(0, 0)
-        moment(0)
+        front("x", 1, 0)
+        middle("x", 0, 1)
+        back_x(0, 1)
         front("x", 1, 1)
+        moment(0)
         middle("x", 1, 0)
-        middle("x", 1, 1)
         back_x(1, 0)
+        middle("x", 1, 1)
         back_x(1, 1)
         moment(1)
         finish(0, [1024])

@@ -26,7 +26,7 @@ LIST_COLS = J_PASS // 16
 ALPHA = 0.04
 BANKS = 5
 V_GATHERS = [("g", 0, 0)]
-V_SUBS = [("g", 0, 1), ("g", 1, 1)]
+V_SUBS = []
 TAGS = {}
 
 
@@ -49,13 +49,11 @@ def tile_list_moment_offset_centred_placed_kernel(tc, xf, ra, ow, gt, rb, old, o
 
         g_list = load("g_list", offs2, U16)
         g_table = [load("g_table0", gt[rows(0), :])]
-        w_rows = keep.tile([P, PASSES * P], F32, name="w_rows")
-        nc.vector.memset(w_rows[:], 0.0)
-        for s, vec in enumerate((ra, rb)):
-            nc.sync.dma_start(
-                w_rows[PACK * s : PACK * (s + 1), :].rearrange("t (b r) -> t b r", r=SET),
-                vec.rearrange("o (b t r) -> t (o b) r", t=PACK, r=SET),
-            )
+        slot_w = []
+        for name, vec in (("ra", ra), ("rb", rb)):
+            wt = keep.tile([P, PASSES, PACK], F32, name="slot_" + name)
+            nc.scalar.dma_start(wt[:], vec.rearrange("o (g p t) -> p (o g) t", p=P, t=PACK))
+            slot_w.append(wt)
         g_table.append(load("g_table1", gt[rows(1), :]))
         x_list = load("x_list", offs, U16)
         def load_own(i, g):
@@ -77,11 +75,6 @@ def tile_list_moment_offset_centred_placed_kernel(tc, xf, ra, ow, gt, rb, old, o
         ident = keep.tile([P, P], F32, name="ident")
         make_identity(nc, ident[:])
 
-        w_bank = psum.tile([P, PASSES, P], F32, name="w_bank")
-        for g in range(PASSES):
-            nc.tensor.transpose(w_bank[:, g, :], w_rows[:, P * g : P * (g + 1)], ident[:])
-        slot_w = keep.tile([P, PASSES, 2 * PACK], F32, name="slot_w")
-        nc.vector.tensor_copy(slot_w[:], w_bank[:, :, 0 : 2 * PACK])
 
         pages = []
         for i in range(2):
@@ -107,35 +100,41 @@ def tile_list_moment_offset_centred_placed_kernel(tc, xf, ra, ow, gt, rb, old, o
                 nc.scalar.activation(picked[:], listed, COPY)
             return picked
 
-        def by_slot(ap):
-            return ap.rearrange("p (b t r) -> p t b r", t=PACK, r=SET)
+        def next_bank():
+            turned.append(None)
+            return bank_ring[(len(turned) - 1) % len(bank_ring)]
 
-        def slots(tile):
-            return tile[:].rearrange("p (t b r) -> p t b r", t=PACK, r=SET)
+        def turn(bank, tile, first, last):
+            for t in range(PACK):
+                nc.tensor.matmul(
+                    bank[:, t, :], tile(t), ident[:], start=(first and t == 0), stop=(last and t == PACK - 1), is_transpose=True
+                )
 
-        def centre(name, picked, eng):
+        def centre(name, picked):
+            bank = next_bank()
+            turn(bank, lambda t: picked[:, t : J_PASS : PACK], True, False)
             sums = new(name + "_sums", [P, J_PASS // SET], F32)
             nc.vector.tensor_reduce(sums[:], picked[:].rearrange("p (c r) -> p c r", r=SET), mybir.AxisListType.X, ALU.add)
-            means = new(name + "_means", [P, J_PASS // SET], F32)
-            eng.tensor_scalar(means[:], sums[:], 1.0 / SET, 0.0, ALU.mult, ALU.add)
+            less = new(name + "_less", [P, P], F32)
+            nc.vector.tensor_scalar(
+                less[:].rearrange("p (c h) -> p c h", h=2),
+                sums[:].rearrange("p (c o) -> p c o", o=1).to_broadcast([P, J_PASS // SET, 2]),
+                -1.0 / SET,
+                None,
+                ALU.mult,
+            )
+            turn(bank, lambda t: less[:], False, True)
+            return bank
+
+        def offset(name, picked, mine):
             diff = new(name, [P, J_PASS], F32)
-            spread = means[:].rearrange("p (b t o) -> p t b o", t=PACK, o=1).to_broadcast([P, PACK, BLOCKS, SET])
-            eng.tensor_tensor(slots(diff), by_slot(picked[:]), spread, ALU.subtract)
-            return diff
-
-        def offset(diff, picked, mine, eng):
-            eng.tensor_tensor(slots(diff), by_slot(picked[:]), by_slot(mine[:]), ALU.subtract)
-            return diff
-
-        def turn(diff):
-            bank = bank_ring[len(turned) % len(bank_ring)]
-            turned.append(diff)
-            for t in range(PACK):
-                nc.tensor.transpose(bank[:, t, :], diff[:, P * t : P * (t + 1)], ident[:])
+            nc.vector.tensor_tensor(diff[:], picked[:], mine[:], ALU.subtract)
+            bank = next_bank()
+            turn(bank, lambda t: diff[:, t : J_PASS : PACK], True, True)
             return bank
 
         def weigh(grouped, bank, g, side):
-            wts = slot_w[:, g : g + 1, PACK * side : PACK * (side + 1)].to_broadcast([P, P, PACK])
+            wts = slot_w[side][:, g : g + 1, :].to_broadcast([P, P, PACK])
             nc.vector.tensor_tensor(grouped, bank[:].rearrange("p t n -> p n t"), wts, ALU.mult)
 
         def quantise(grouped, codes, scales):
@@ -172,12 +171,10 @@ def tile_list_moment_offset_centred_placed_kernel(tc, xf, ra, ow, gt, rb, old, o
         def front(side, i, g):
             unit = (side, i, g)
             name = "%s%d%d" % unit
-            eng = nc.vector if unit in V_SUBS else nc.gpsimd
             if side == "g":
-                diff = centre("diff_" + name, gather("picked_" + name, g_table[i], g_list, g, unit in V_GATHERS), eng)
+                banks[unit] = centre("centre_" + name, gather("picked_" + name, g_table[i], g_list, g, unit in V_GATHERS))
             else:
-                diff = offset(new("diff_" + name, [P, J_PASS], F32), gather("picked_" + name, x_table[i], x_list, g, unit in V_GATHERS), own[i][g], eng)
-            banks[unit] = turn(diff)
+                banks[unit] = offset("diff_" + name, gather("picked_" + name, x_table[i], x_list, g, unit in V_GATHERS), own[i][g])
 
         def middle(side, i, g):
             if side == "g":
@@ -198,22 +195,22 @@ def tile_list_moment_offset_centred_placed_kernel(tc, xf, ra, ow, gt, rb, old, o
         front("g", 0, 0)
         front("g", 0, 1)
         front("g", 1, 0)
-        middle("g", 0, 1)
         middle("g", 0, 0)
         front("g", 1, 1)
+        middle("g", 0, 1)
         front("x", 0, 0)
         middle("g", 1, 0)
-        back_g(0)
         front("x", 0, 1)
+        back_g(0)
         middle("g", 1, 1)
-        middle("x", 0, 0)
-        back_g(1)
-        back_x(0, 0)
         front("x", 1, 0)
+        back_g(1)
+        middle("x", 0, 0)
+        back_x(0, 0)
         middle("x", 0, 1)
         back_x(0, 1)
-        front("x", 1, 1)
         moment(0)
+        front("x", 1, 1)
         middle("x", 1, 0)
         back_x(1, 0)
         middle("x", 1, 1)

@@ -3,7 +3,7 @@ from contextlib import ExitStack
 import concourse.mybir as mybir
 from concourse.masks import make_identity
 
-K, J, N, T, V, Q = 256, 1024, 256, 2048, 2048, 1024
+K, J, N, Q = 256, 1024, 256, 1024
 FLOPS = 2 * K * J * N
 
 F32 = mybir.dt.float32
@@ -21,13 +21,10 @@ PACK = 4
 J_PASS = P * PACK
 PASSES = J // J_PASS
 SET = 8
-BLOCKS = J_PASS // 32
 LIST_COLS = J_PASS // 16
 ALPHA = 0.04
-BANKS = 5
-V_GATHERS = [("g", 0, 0)]
-V_SUBS = []
-TAGS = {}
+RING = 4
+LAST_WIDTHS = (512, 256, 256)
 
 
 def tile_list_moment_offset_centred_placed_kernel(tc, xf, ra, ow, gt, rb, old, offs, offs2, offs3, out):
@@ -37,184 +34,153 @@ def tile_list_moment_offset_centred_placed_kernel(tc, xf, ra, ow, gt, rb, old, o
         psum = ctx.enter_context(tc.psum_pool(name="psum", bufs=1))
 
         def new(name, shape, dtype):
-            return keep.tile(shape, dtype, name=name, tag=TAGS.get(name, name), align_bytes=64)
+            return keep.tile(shape, dtype, name=name, align_bytes=64)
 
         def load(name, src, dtype=F32):
-            t = keep.tile(list(src.shape), dtype, name=name, align_bytes=64)
-            nc.sync.dma_start(t[:], src)
-            return t
+            dst = new(name, list(src.shape), dtype)
+            nc.sync.dma_start(dst[:], src)
+            return dst
 
-        def rows(i):
+        def block(i):
             return slice(P * i, P * (i + 1))
 
+        def slots(g):
+            return slice(J_PASS * g, J_PASS * (g + 1))
+
+        def by_partition(vec):
+            return vec.rearrange("o (g p t) -> p (o g) t", p=P, t=PACK)
+
         g_list = load("g_list", offs2, U16)
-        g_table = [load("g_table0", gt[rows(0), :])]
-        slot_w = []
-        for name, vec in (("ra", ra), ("rb", rb)):
-            wt = keep.tile([P, PASSES, PACK], F32, name="slot_" + name)
-            nc.scalar.dma_start(wt[:], vec.rearrange("o (g p t) -> p (o g) t", p=P, t=PACK))
-            slot_w.append(wt)
-        g_table.append(load("g_table1", gt[rows(1), :]))
+        g_table = [load("g_table%d" % i, gt[block(i), :]) for i in range(2)]
+        g_weight = load("g_weight", by_partition(rb))
         x_list = load("x_list", offs, U16)
-        def load_own(i, g):
-            return load("own%d_%d" % (i, g), ow[rows(i), J_PASS * g : J_PASS * (g + 1)])
-
-        x_table = [load("x_table0", xf[rows(0), :])]
-        own = [[load_own(0, 0)]]
-        x_table.append(load("x_table1", xf[rows(1), :]))
-        own[0].append(load_own(0, 1))
-        own.append([load_own(1, g) for g in range(PASSES)])
+        x_table = [load("x_table0", xf[block(0), :])]
+        x_weight = load("x_weight", by_partition(ra))
+        own = {(0, 0): load("own00", ow[block(0), slots(0)])}
+        x_table.append(load("x_table1", xf[block(1), :]))
+        for i, g in ((0, 1), (1, 0), (1, 1)):
+            own[i, g] = load("own%d%d" % (i, g), ow[block(i), slots(g)])
         place_list = load("place_list", offs3, U16)
-        store_old = [load("store_old%d" % i, old[rows(i), :]) for i in range(2)]
+        store_old = [load("store_old%d" % i, old[block(i), :]) for i in range(2)]
 
-        warm_in = keep.tile([P, 1], F32, name="warm_in")
-        warm_out = keep.tile([P, 1], F32, name="warm_out")
+        warm_in = new("warm_in", [P, 1], F32)
+        warm_out = new("warm_out", [P, 1], F32)
         nc.vector.memset(warm_in[:], 0.0)
         nc.scalar.activation(warm_out[:], warm_in[:], COPY)
 
-        ident = keep.tile([P, P], F32, name="ident")
+        ident = new("ident", [P, P], F32)
         make_identity(nc, ident[:])
 
-
-        pages = []
-        for i in range(2):
-            page = keep.tile([P, Q], F32, name="page%d" % i)
+        pages = [new("page%d" % i, [P, Q], F32) for i in range(2)]
+        for page in pages:
             nc.vector.memset(page[:], 0.0)
-            pages.append(page)
 
-        g_grouped = [new("g_grouped%d" % g, [P, N, PACK], BF16) for g in range(PASSES)]
-        g_codes = [new("g_codes%d" % g, [P, N], U32) for g in range(PASSES)]
-        g_scales = [new("g_scales%d" % g, [P, N], U8) for g in range(PASSES)]
-        res0 = new("res0", [P, Q], F32)
-        bank_ring = [psum.tile([P, PACK, P], F32, name="bank%d" % b) for b in range(4)]
-        turned = []
-        u_codes = {}
-        u_scales = {}
+        ring = [psum.tile([P, PACK, P], F32, name="bank%d" % b) for b in range(RING)]
 
-        def gather(name, table, lst, g, on_vector):
-            picked = new(name, [P, J_PASS], F32)
-            listed = table[:].indirect(lst[:, LIST_COLS * g : LIST_COLS * (g + 1)])
+        def gather(picked, table, entries, g, on_vector=False):
+            listed = table[:].indirect(entries[:, LIST_COLS * g : LIST_COLS * (g + 1)])
             if on_vector:
-                nc.vector.tensor_copy(picked[:], listed)
+                nc.vector.tensor_copy(picked, listed)
             else:
-                nc.scalar.activation(picked[:], listed, COPY)
-            return picked
+                nc.scalar.activation(picked, listed, COPY)
 
-        def next_bank():
-            turned.append(None)
-            return bank_ring[(len(turned) - 1) % len(bank_ring)]
-
-        def turn(bank, tile, first, last):
+        def turn(bank, columns, opens, closes):
             for t in range(PACK):
                 nc.tensor.matmul(
-                    bank[:, t, :], tile(t), ident[:], start=(first and t == 0), stop=(last and t == PACK - 1), is_transpose=True
+                    bank[:, t, :],
+                    columns(t),
+                    ident[:],
+                    start=(opens and t == 0),
+                    stop=(closes and t == PACK - 1),
+                    is_transpose=True,
                 )
 
-        def centre(name, picked):
-            bank = next_bank()
-            turn(bank, lambda t: picked[:, t : J_PASS : PACK], True, False)
-            sums = new(name + "_sums", [P, J_PASS // SET], F32)
+        def every_4th(tile):
+            return lambda t: tile[:, t:J_PASS:PACK]
+
+        def centred(i):
+            picked = new("g_picked%d" % i, [P, J], F32)
+            for g in range(PASSES):
+                gather(picked[:, slots(g)], g_table[i], g_list, g, on_vector=(i, g) == (0, 0))
+                turn(ring[PASSES * i + g], every_4th(picked[:, slots(g)]), True, False)
+            sums = new("g_sums%d" % i, [P, J // SET], F32)
             nc.vector.tensor_reduce(sums[:], picked[:].rearrange("p (c r) -> p c r", r=SET), mybir.AxisListType.X, ALU.add)
-            less = new(name + "_less", [P, P], F32)
+            less = new("g_less%d" % i, [P, PASSES * P], F32)
             nc.vector.tensor_scalar(
                 less[:].rearrange("p (c h) -> p c h", h=2),
-                sums[:].rearrange("p (c o) -> p c o", o=1).to_broadcast([P, J_PASS // SET, 2]),
+                sums[:].rearrange("p (c o) -> p c o", o=1).to_broadcast([P, J // SET, 2]),
                 -1.0 / SET,
                 None,
                 ALU.mult,
             )
-            turn(bank, lambda t: less[:], False, True)
-            return bank
+            for g in range(PASSES):
+                turn(ring[PASSES * i + g], lambda t: less[:, block(g)], False, True)
 
-        def offset(name, picked, mine):
-            diff = new(name, [P, J_PASS], F32)
-            nc.vector.tensor_tensor(diff[:], picked[:], mine[:], ALU.subtract)
-            bank = next_bank()
-            turn(bank, lambda t: diff[:, t : J_PASS : PACK], True, True)
-            return bank
+        def offset(i, g):
+            picked = new("x_picked%d%d" % (i, g), [P, J_PASS], F32)
+            gather(picked[:], x_table[i], x_list, g)
+            diff = new("x_diff%d%d" % (i, g), [P, J_PASS], F32)
+            nc.vector.tensor_tensor(diff[:], picked[:], own[i, g][:], ALU.subtract)
+            turn(ring[PASSES * i + g], every_4th(diff), True, True)
 
-        def weigh(grouped, bank, g, side):
-            wts = slot_w[side][:, g : g + 1, :].to_broadcast([P, P, PACK])
-            nc.vector.tensor_tensor(grouped, bank[:].rearrange("p t n -> p n t"), wts, ALU.mult)
+        def weigh(grouped, i, g, weight):
+            spread = weight[:, g : g + 1, :].to_broadcast([P, P, PACK])
+            nc.vector.tensor_tensor(grouped, ring[PASSES * i + g][:].rearrange("p t n -> p n t"), spread, ALU.mult)
 
-        def quantise(grouped, codes, scales):
-            nc.vector.quantize_mx(out=codes, scales=scales, in_=grouped.rearrange("p n t -> p (n t)"))
+        def quantise(name, grouped, fmt):
+            width = grouped.shape[1]
+            codes = new(name + "_codes", [P, width], U32)
+            scales = new(name + "_scales", [P, width], U8)
+            nc.vector.quantize_mx(out=codes[:].bitcast(fmt), scales=scales[:], in_=grouped.rearrange("p n t -> p (n t)"))
+            return codes, scales
 
-        def moment(i):
+        def moment(i, u_ops, g_ops):
             acc = psum.tile([P, N], F32, name="acc%d" % i)
             for g in range(PASSES):
                 nc.tensor.matmul_mx(
                     out=acc[:],
-                    lhsT=u_codes[i, g][:].bitcast(E4M3X4),
-                    lhsT_scale=u_scales[i, g][:],
-                    rhs=g_codes[g][:].bitcast(E5M2X4),
-                    rhs_scale=g_scales[g][:],
+                    lhsT=u_ops[g][0].bitcast(E4M3X4),
+                    lhsT_scale=u_ops[g][1],
+                    rhs=g_ops[g][0].bitcast(E5M2X4),
+                    rhs_scale=g_ops[g][1],
                     start=(g == 0),
                     stop=(g == PASSES - 1),
                 )
-            w = keep.tile([P, N], F32, name="w%d" % i)
+            w = new("w%d" % i, [P, N], F32)
             nc.scalar.activation(w[:], acc[:], COPY)
             nc.scalar.activation(pages[i][:].indirect(place_list[:]), w[:], COPY)
 
-        def finish(i, widths):
-            c0 = 0
-            for h, width in enumerate(widths):
-                cols = slice(c0, c0 + width)
-                c0 = c0 + width
-                res = res0 if i == 0 else new("res%d_%d" % (i, h), [P, width], F32)
-                nc.vector.scalar_tensor_tensor(res[:], pages[i][:, cols], ALPHA, store_old[i][:, cols], ALU.mult, ALU.add)
-                nc.sync.dma_start(out[rows(i), cols], res[:])
+        def finish(res, i, cols):
+            nc.vector.scalar_tensor_tensor(res, pages[i][:, cols], ALPHA, store_old[i][:, cols], ALU.mult, ALU.add)
+            nc.sync.dma_start(out[block(i), cols], res)
 
-        banks = {}
-        grouped = {}
+        g_grouped = [new("g_grouped%d" % g, [P, N, PACK], BF16) for g in range(PASSES)]
+        res0 = new("res0", [P, Q], F32)
+        x_grouped = res0[:, 0:J_PASS].bitcast(BF16).rearrange("p (n t) -> p n t", t=PACK)
 
-        def front(side, i, g):
-            unit = (side, i, g)
-            name = "%s%d%d" % unit
-            if side == "g":
-                banks[unit] = centre("centre_" + name, gather("picked_" + name, g_table[i], g_list, g, unit in V_GATHERS))
-            else:
-                banks[unit] = offset("diff_" + name, gather("picked_" + name, x_table[i], x_list, g, unit in V_GATHERS), own[i][g])
+        centred(0)
+        centred(1)
+        for g in range(PASSES):
+            weigh(g_grouped[g][:, block(0), :], 0, g, g_weight)
+        offset(0, 0)
+        weigh(g_grouped[0][:, block(1), :], 1, 0, g_weight)
+        offset(0, 1)
+        weigh(g_grouped[1][:, block(1), :], 1, 1, g_weight)
+        g_ops = [[part[:] for part in quantise("g%d" % g, g_grouped[g][:], E5M2X4)] for g in range(PASSES)]
+        for g in range(PASSES):
+            offset(1, g)
+        for g in range(PASSES):
+            weigh(x_grouped[:, block(g), :], 0, g, x_weight)
+        codes, scales = quantise("u0", x_grouped, E4M3X4)
+        moment(0, [(codes[:, block(g)], scales[:, block(g)]) for g in range(PASSES)], g_ops)
+        u_ops = []
+        for g in range(PASSES):
+            weigh(x_grouped[:, block(g), :], 1, g, x_weight)
+            u_ops.append([part[:] for part in quantise("u1%d" % g, x_grouped[:, block(g), :], E4M3X4)])
+        moment(1, u_ops, g_ops)
 
-        def middle(side, i, g):
-            if side == "g":
-                weigh(g_grouped[g][:, rows(i), :], banks[side, i, g], g, 1)
-            else:
-                host = new("grouped_x%d%d" % (i, g), [P, J_PASS // 2], F32) if (i, g) != (1, 1) else res0
-                grouped[i, g] = host[:, 0 : J_PASS // 2].bitcast(BF16).rearrange("p (n t) -> p n t", t=PACK)
-                weigh(grouped[i, g], banks[side, i, g], g, 0)
-
-        def back_g(g):
-            quantise(g_grouped[g][:], g_codes[g][:].bitcast(E5M2X4), g_scales[g][:])
-
-        def back_x(i, g):
-            u_codes[i, g] = new("u_codes%d_%d" % (i, g), [P, P], U32)
-            u_scales[i, g] = new("u_scales%d_%d" % (i, g), [P, P], U8)
-            quantise(grouped[i, g], u_codes[i, g][:].bitcast(E4M3X4), u_scales[i, g][:])
-
-        front("g", 0, 0)
-        front("g", 0, 1)
-        front("g", 1, 0)
-        middle("g", 0, 0)
-        front("g", 1, 1)
-        middle("g", 0, 1)
-        front("x", 0, 0)
-        middle("g", 1, 0)
-        front("x", 0, 1)
-        back_g(0)
-        middle("g", 1, 1)
-        front("x", 1, 0)
-        back_g(1)
-        middle("x", 0, 0)
-        back_x(0, 0)
-        middle("x", 0, 1)
-        back_x(0, 1)
-        moment(0)
-        front("x", 1, 1)
-        middle("x", 1, 0)
-        back_x(1, 0)
-        middle("x", 1, 1)
-        back_x(1, 1)
-        moment(1)
-        finish(0, [1024])
-        finish(1, [512, 256, 256])
+        finish(res0[:], 0, slice(0, Q))
+        start = 0
+        for h, width in enumerate(LAST_WIDTHS):
+            finish(new("res1%d" % h, [P, width], F32)[:], 1, slice(start, start + width))
+            start = start + width

from contextlib import ExitStack

import concourse.mybir as mybir
from concourse.masks import make_identity

K, J, N, Q = 256, 1024, 256, 1024
FLOPS = 2 * K * J * N

F32 = mybir.dt.float32
BF16 = mybir.dt.bfloat16
U32 = mybir.dt.uint32
U16 = mybir.dt.uint16
U8 = mybir.dt.uint8
E4M3X4 = mybir.dt.float8_e4m3fn_x4
E5M2X4 = mybir.dt.float8_e5m2_x4
ALU = mybir.AluOpType
COPY = mybir.ActivationFunctionType.Copy

P = 128
PACK = 4
J_PASS = P * PACK
PASSES = J // J_PASS
SET = 8
LIST_COLS = J_PASS // 16
ALPHA = 0.04
RING = 4
LAST_WIDTHS = (512, 256, 256)


def tile_list_moment_offset_centred_placed_kernel(tc, xf, ra, ow, gt, rb, old, offs, offs2, offs3, out):
    nc = tc.nc
    with ExitStack() as ctx:
        keep = ctx.enter_context(tc.tile_pool(name="keep", bufs=1))
        psum = ctx.enter_context(tc.psum_pool(name="psum", bufs=1))

        def new(name, shape, dtype):
            return keep.tile(shape, dtype, name=name, align_bytes=64)

        def load(name, src, dtype=F32):
            dst = new(name, list(src.shape), dtype)
            nc.sync.dma_start(dst[:], src)
            return dst

        def block(i):
            return slice(P * i, P * (i + 1))

        def slots(g):
            return slice(J_PASS * g, J_PASS * (g + 1))

        def by_partition(vec):
            return vec.rearrange("o (g p t) -> p (o g) t", p=P, t=PACK)

        g_list = load("g_list", offs2, U16)
        g_table = [load("g_table%d" % i, gt[block(i), :]) for i in range(2)]
        g_weight = load("g_weight", by_partition(rb))
        x_list = load("x_list", offs, U16)
        x_table = [load("x_table0", xf[block(0), :])]
        x_weight = load("x_weight", by_partition(ra))
        own = {(0, 0): load("own00", ow[block(0), slots(0)])}
        x_table.append(load("x_table1", xf[block(1), :]))
        for i, g in ((0, 1), (1, 0), (1, 1)):
            own[i, g] = load("own%d%d" % (i, g), ow[block(i), slots(g)])
        place_list = load("place_list", offs3, U16)
        store_old = [load("store_old%d" % i, old[block(i), :]) for i in range(2)]

        warm_in = new("warm_in", [P, 1], F32)
        warm_out = new("warm_out", [P, 1], F32)
        nc.vector.memset(warm_in[:], 0.0)
        nc.scalar.activation(warm_out[:], warm_in[:], COPY)

        ident = new("ident", [P, P], F32)
        make_identity(nc, ident[:])

        pages = [new("page%d" % i, [P, Q], F32) for i in range(2)]
        for page in pages:
            nc.vector.memset(page[:], 0.0)

        ring = [psum.tile([P, PACK, P], F32, name="bank%d" % b) for b in range(RING)]

        def gather(picked, table, entries, g, on_vector=False):
            listed = table[:].indirect(entries[:, LIST_COLS * g : LIST_COLS * (g + 1)])
            if on_vector:
                nc.vector.tensor_copy(picked, listed)
            else:
                nc.scalar.activation(picked, listed, COPY)

        def turn(bank, columns, opens, closes):
            for t in range(PACK):
                nc.tensor.matmul(
                    bank[:, t, :],
                    columns(t),
                    ident[:],
                    start=(opens and t == 0),
                    stop=(closes and t == PACK - 1),
                    is_transpose=True,
                )

        def every_4th(tile):
            return lambda t: tile[:, t:J_PASS:PACK]

        def centred(i):
            picked = new("g_picked%d" % i, [P, J], F32)
            for g in range(PASSES):
                gather(picked[:, slots(g)], g_table[i], g_list, g, on_vector=(i, g) == (0, 0))
                turn(ring[PASSES * i + g], every_4th(picked[:, slots(g)]), True, False)
            sums = new("g_sums%d" % i, [P, J // SET], F32)
            nc.vector.tensor_reduce(sums[:], picked[:].rearrange("p (c r) -> p c r", r=SET), mybir.AxisListType.X, ALU.add)
            less = new("g_less%d" % i, [P, PASSES * P], F32)
            nc.vector.tensor_scalar(
                less[:].rearrange("p (c h) -> p c h", h=2),
                sums[:].rearrange("p (c o) -> p c o", o=1).to_broadcast([P, J // SET, 2]),
                -1.0 / SET,
                None,
                ALU.mult,
            )
            for g in range(PASSES):
                turn(ring[PASSES * i + g], lambda t: less[:, block(g)], False, True)

        def offset(i, g):
            picked = new("x_picked%d%d" % (i, g), [P, J_PASS], F32)
            gather(picked[:], x_table[i], x_list, g)
            diff = new("x_diff%d%d" % (i, g), [P, J_PASS], F32)
            nc.vector.tensor_tensor(diff[:], picked[:], own[i, g][:], ALU.subtract)
            turn(ring[PASSES * i + g], every_4th(diff), True, True)

        def weigh(grouped, i, g, weight):
            spread = weight[:, g : g + 1, :].to_broadcast([P, P, PACK])
            nc.vector.tensor_tensor(grouped, ring[PASSES * i + g][:].rearrange("p t n -> p n t"), spread, ALU.mult)

        def quantise(name, grouped, fmt):
            width = grouped.shape[1]
            codes = new(name + "_codes", [P, width], U32)
            scales = new(name + "_scales", [P, width], U8)
            nc.vector.quantize_mx(out=codes[:].bitcast(fmt), scales=scales[:], in_=grouped.rearrange("p n t -> p (n t)"))
            return codes, scales

        def moment(i, u_ops, g_ops):
            acc = psum.tile([P, N], F32, name="acc%d" % i)
            for g in range(PASSES):
                nc.tensor.matmul_mx(
                    out=acc[:],
                    lhsT=u_ops[g][0].bitcast(E4M3X4),
                    lhsT_scale=u_ops[g][1],
                    rhs=g_ops[g][0].bitcast(E5M2X4),
                    rhs_scale=g_ops[g][1],
                    start=(g == 0),
                    stop=(g == PASSES - 1),
                )
            w = new("w%d" % i, [P, N], F32)
            nc.scalar.activation(w[:], acc[:], COPY)
            nc.scalar.activation(pages[i][:].indirect(place_list[:]), w[:], COPY)

        def finish(res, i, cols):
            nc.vector.scalar_tensor_tensor(res, pages[i][:, cols], ALPHA, store_old[i][:, cols], ALU.mult, ALU.add)
            nc.sync.dma_start(out[block(i), cols], res)

        g_grouped = [new("g_grouped%d" % g, [P, N, PACK], BF16) for g in range(PASSES)]
        res0 = new("res0", [P, Q], F32)
        x_grouped = res0[:, 0:J_PASS].bitcast(BF16).rearrange("p (n t) -> p n t", t=PACK)

        centred(0)
        centred(1)
        for g in range(PASSES):
            weigh(g_grouped[g][:, block(0), :], 0, g, g_weight)
        offset(0, 0)
        weigh(g_grouped[0][:, block(1), :], 1, 0, g_weight)
        offset(0, 1)
        weigh(g_grouped[1][:, block(1), :], 1, 1, g_weight)
        g_ops = [[part[:] for part in quantise("g%d" % g, g_grouped[g][:], E5M2X4)] for g in range(PASSES)]
        for g in range(PASSES):
            offset(1, g)
        for g in range(PASSES):
            weigh(x_grouped[:, block(g), :], 0, g, x_weight)
        codes, scales = quantise("u0", x_grouped, E4M3X4)
        moment(0, [(codes[:, block(g)], scales[:, block(g)]) for g in range(PASSES)], g_ops)
        u_ops = []
        for g in range(PASSES):
            weigh(x_grouped[:, block(g), :], 1, g, x_weight)
            u_ops.append([part[:] for part in quantise("u1%d" % g, x_grouped[:, block(g), :], E4M3X4)])
        moment(1, u_ops, g_ops)

        finish(res0[:], 0, slice(0, Q))
        start = 0
        for h, width in enumerate(LAST_WIDTHS):
            finish(new("res1%d" % h, [P, width], F32)[:], 1, slice(start, start + width))
            start = start + width
